import numpy as np
import ml_dtypes


def mxq(x, axis, fmt="e4m3"):
    dtype, down = {"e4m3": (ml_dtypes.float8_e4m3fn, 7), "e5m2": (ml_dtypes.float8_e5m2, 14)}[fmt]
    v = np.moveaxis(np.asarray(x, np.float32).astype(ml_dtypes.bfloat16).astype(np.float64), axis, -1)
    blocks = v.reshape(v.shape[:-1] + (-1, 32))
    amax = np.abs(blocks).max(-1, keepdims=True)
    byte = np.maximum(np.where(amax > 0, np.frexp(amax)[1] - 1 + 127, 0) - down, 1)
    scale = np.exp2(byte - 127.0)
    codes = (blocks / scale).astype(np.float32).astype(dtype).astype(np.float64)
    return np.moveaxis((codes * scale).reshape(v.shape), -1, axis)


WIDE = False


def mx_kscale(k):
    if not WIDE:
        return np.ones(k)
    levels = np.array([10, -10, 5, -5, 0])
    if k % 512:
        return np.exp2(np.random.permutation(np.resize(levels, k // 32))).repeat(32)
    a = np.empty((k // 512, 16))
    for p in range(k // 512):
        a[p, :8] = np.random.permutation(np.resize(levels, 8))
        for g in range(8):
            far = levels[np.abs(levels - a[p, g]) >= 10]
            a[p, g + 8] = far[np.random.randint(len(far))]
    return np.exp2(a.ravel()).repeat(32)


def f64(x):
    return np.asarray(x).astype(np.float64)


def striped(idx):
    return np.tile(idx.reshape(-1, 16).T, (8, 1)).astype(np.uint16)


def unstriped(offs):
    return offs[:16].T.reshape(-1).astype(np.int64)


E2M1 = np.array([0.0, 0.5, 1.0, 1.5, 2.0, 3.0, 4.0, 6.0, -0.0, -0.5, -1.0, -1.5, -2.0, -3.0, -4.0, -6.0])


def pack_weight(w, fmt):
    k, n = w.shape
    w = f64(np.asarray(w, np.float32).astype(ml_dtypes.bfloat16)).reshape(k // 32, 32, n)
    amax = np.abs(w).max(1)
    if fmt == "e4m3":
        byte = np.frexp(amax)[1] - 1 + 127 - 7
    else:
        mant, ex = np.frexp(amax / 6.0)
        byte = np.where(mant > 0.5, ex, ex - 1) + 127
    byte = np.clip(np.where(amax > 0, byte, 1), 1, 254)
    scaled = (w * np.exp2(127.0 - byte)[:, None, :]).reshape(k, n).astype(np.float32)
    by_word = np.ascontiguousarray(scaled.reshape(k // 512, 128, 4, n).transpose(0, 1, 3, 2))
    if fmt == "e4m3":
        words = by_word.astype(ml_dtypes.float8_e4m3fn).view(np.uint8)
    else:
        c = by_word.astype(ml_dtypes.float4_e2m1fn).view(np.uint8) & 0xF
        words = (c[..., 0::2] | (c[..., 1::2] << 4)).reshape(k // 512, 128, 2 * n)
    return np.ascontiguousarray(words), np.ascontiguousarray(byte.astype(np.uint8).reshape(k // 512, 16, n))


def unpack_weight(words, scales, fmt):
    g, _, n = scales.shape
    words = np.ascontiguousarray(words).reshape(g, 128, n, -1)
    if fmt == "e4m3":
        vals = words.view(ml_dtypes.float8_e4m3fn).astype(np.float64)
    else:
        nib = np.empty((g, 128, n, 4), np.uint8)
        nib[..., 0::2] = words & 0xF
        nib[..., 1::2] = words >> 4
        vals = E2M1[nib]
    vals = vals * np.repeat(np.exp2(scales.astype(np.float64) - 127.0), 8, axis=1)[..., None]
    return vals.transpose(0, 1, 3, 2).reshape(g * 512, n)


def gelu(v):
    return 0.5 * v * (1.0 + np.tanh(np.sqrt(2.0 / np.pi) * (v + 0.044715 * v**3)))


K, T, S, P, H, N = 512, 4096, 1024, 512, 1024, 384


def setup_inputs():
    n = np.random.standard_normal
    s = mx_kscale(K)[:, None]
    u = mx_kscale(H)[:, None]
    perm = np.random.permutation(S)
    tab_words, tab_scales = pack_weight(n((K, T)) * s, "e4m3")
    w2_words, w2_scales = pack_weight(0.5 * n((K, H)) / np.sqrt(K) / s, "e2m1")
    w4_words, w4_scales = pack_weight(n((H, N)) / np.sqrt(H) / u, "e4m3")
    return {
        "tab_words": tab_words,
        "tab_scales": tab_scales,
        "offs": striped(np.random.permutation(T)[:S]),
        "pos1": striped(perm[:P]),
        "pos2": striped(perm[P:]),
        "w1": (0.6 * n((K, H)) / np.sqrt(K) / s).astype(np.float32),
        "w2_words": w2_words,
        "w2_scales": w2_scales,
        "w3": (0.65 * n((K, H)) / np.sqrt(K) / s).astype(np.float32),
        "mend": (5.0 * n((H, P))).astype(np.float32),
        "skip": np.random.uniform(0.5, 1.5, H).astype(np.float32),
        "wgs": np.exp(0.3 * n((128, P))).astype(np.float32),
        "gain": (np.random.uniform(0.5, 2.0, H) * u[:, 0]).astype(np.float32),
        "w4_words": w4_words,
        "w4_scales": w4_scales,
    }


def reference(tab_words, tab_scales, offs, pos1, pos2, w1, w2_words, w2_scales, w3, mend, skip, wgs, gain, w4_words, w4_scales):
    v = unpack_weight(tab_words, tab_scales, "e4m3")[:, unstriped(offs)]
    w2 = unpack_weight(w2_words, w2_scales, "e2m1")
    w4 = unpack_weight(w4_words, w4_scales, "e4m3")
    hit = mxq(f64(w1), 0, "e4m3").T @ v
    ring = w2.T @ v
    base = mxq(f64(w3), 0, "e4m3").T @ v
    h = hit * ring + base
    top = h.max(axis=1)
    a = np.exp(h[:, unstriped(pos1)] - top[:, None]) * f64(mend)
    page = f64(skip)[:, None] * h
    page[:, unstriped(pos2)] = np.tile(f64(wgs), (H // 128, 1)) * a
    q = mxq(f64(gain)[:, None] * page, 0, "e4m3")
    return w4.T @ q

@@ -1,0 +1,272 @@
+from contextlib import ExitStack
+
+import concourse.mybir as mybir
+
+K, T, S, LOOK, H, N = 512, 4096, 1024, 512, 1024, 384
+FLOPS = 2 * (3 * K * H * S + H * N * S)
+
+F32 = mybir.dt.float32
+BF16 = mybir.dt.bfloat16
+I32 = mybir.dt.int32
+U32 = mybir.dt.uint32
+U16 = mybir.dt.uint16
+U8 = mybir.dt.uint8
+FP8X4 = mybir.dt.float8_e4m3fn_x4
+FP4X4 = mybir.dt.float4_e2m1fn_x4
+ALU = mybir.AluOpType
+ACT = mybir.ActivationFunctionType
+AX = mybir.AxisListType
+
+P = 128
+PACK = 4
+PASS = P * PACK
+BANK = 512
+GROUPS = H // PASS
+SLOTS = GROUPS * PACK
+HALVES = S // BANK
+BANKS = 8
+
+
+def tile_list_grainloss_window_mender_kernel(
+    tc, tab_words, tab_scales, offs, pos1, pos2, w1, w2_words, w2_scales, w3, mend, skip, wgs, gain, w4_words, w4_scales, out
+):
+    nc = tc.nc
+    with ExitStack() as ctx:
+        keep = ctx.enter_context(tc.tile_pool(name="keep", bufs=1))
+        work = ctx.enter_context(tc.tile_pool(name="work", bufs=2))
+        psum = ctx.enter_context(tc.psum_pool(name="psum", bufs=1))
+        bank_turn = []
+
+        def next_bank():
+            tag = "bank%d" % (len(bank_turn) % BANKS)
+            bank_turn.append(tag)
+            return psum.tile([P, BANK], F32, name=tag, tag=tag)
+
+        def load_scale_rows(queue, plane, rows):
+            by_row = rows.rearrange("a (Q r) c -> r Q a c", r=4)
+            for r in range(4):
+                queue.dma_start(out=plane[r:P:32, :].rearrange("p (a c) -> p a c", a=rows.shape[0]).bitcast(I32), in_=by_row[r].bitcast(I32))
+
+        idx = keep.tile([P, S // 16], U16, name="idx")
+        p1 = keep.tile([P, LOOK // 16], U16, name="p1")
+        p2 = keep.tile([P, LOOK // 16], U16, name="p2")
+        table = keep.tile([P, T], U32, name="table", align_bytes=64)
+        table_sc = keep.tile([P, T], U8, name="table_sc", align_bytes=64)
+        w2_raw = keep.tile([P, 2 * H], U8, name="w2_raw", align_bytes=64)
+        w2_sc_raw = keep.tile([P, H], U8, name="w2_sc_raw", align_bytes=64)
+        w4_codes = keep.tile([P, GROUPS, N], U32, name="w4_codes", align_bytes=64)
+        w4_sc = keep.tile([P, GROUPS * N], U8, name="w4_sc", align_bytes=64)
+
+        nc.vector.memset(table_sc[:].bitcast(I32), 0)
+        nc.vector.memset(w2_sc_raw[:].bitcast(I32), 0)
+        nc.vector.memset(w4_sc[:].bitcast(I32), 0)
+
+        nc.sync.dma_start(out=w2_raw[:].bitcast(I32), in_=w2_words[0].bitcast(I32))
+        load_scale_rows(nc.gpsimd, table_sc, tab_scales)
+        load_scale_rows(nc.gpsimd, w2_sc_raw, w2_scales)
+        nc.sync.dma_start(idx[:], offs)
+        nc.sync.dma_start(out=table[:].bitcast(I32), in_=tab_words[0].rearrange("p t i -> p (t i)").bitcast(I32))
+
+        raw = {}
+
+        def load_weight(name, w, b):
+            for piece in range(2):
+                c0 = PASS * b + 256 * piece
+                tile = keep.tile([P, PACK, 256], F32, name="raw_%s_%d_%d" % (name, b, piece))
+                nc.sync.dma_start(out=tile[:], in_=w[:, c0 : c0 + 256].rearrange("(p j) c -> p j c", j=PACK))
+                raw[name, b, piece] = tile
+
+        load_weight("w1", w1, 0)
+        load_weight("w3", w3, 0)
+        nc.sync.dma_start(p1[:], pos1)
+        nc.sync.dma_start(p2[:], pos2)
+        skip_col = keep.tile([P, GROUPS, PACK], F32, name="skip_col")
+        gain_col = keep.tile([P, GROUPS, PACK], F32, name="gain_col")
+        nc.sync.dma_start(out=skip_col[:], in_=skip.rearrange("(b p t) -> p b t", b=GROUPS, t=PACK))
+        nc.sync.dma_start(out=gain_col[:], in_=gain.rearrange("(b p t) -> p b t", b=GROUPS, t=PACK))
+        wgs_rows = keep.tile([P, PACK, LOOK], F32, name="wgs_rows")
+        for q in range(4):
+            nc.sync.dma_start(out=wgs_rows[32 * q : 32 * q + 32, :, :], in_=wgs.rearrange("(x t) m -> x t m", t=PACK))
+        mend_rows = []
+        for b in range(GROUPS):
+            tile = keep.tile([P, PACK, LOOK], F32, name="mend_%d" % b)
+            mend_rows.append(tile)
+        nc.sync.dma_start(out=mend_rows[0][:], in_=mend[0:PASS, :].rearrange("(p t) m -> p t m", t=PACK))
+        load_weight("w1", w1, 1)
+        load_weight("w3", w3, 1)
+        nc.sync.dma_start(out=mend_rows[1][:], in_=mend[PASS : 2 * PASS, :].rearrange("(p t) m -> p t m", t=PACK))
+        nc.sync.dma_start(out=w4_codes[:].bitcast(I32), in_=w4_words.rearrange("a p c i -> p a (c i)").bitcast(I32))
+        load_scale_rows(nc.sync, w4_sc, w4_scales)
+
+        w2_codes = keep.tile([P, 2 * H], U8, name="w2_codes", align_bytes=64)
+        w2_sc = keep.tile([P, H], U8, name="w2_sc", align_bytes=64)
+        nc.vector.tensor_copy(
+            out=w2_codes[:].rearrange("p (b t m e) -> p b m t e", b=GROUPS, t=PACK, e=2),
+            in_=w2_raw[:].rearrange("p (b m t e) -> p b m t e", b=GROUPS, t=PACK, e=2),
+        )
+
+        v_codes, v_sc = [], []
+        for half in range(HALVES):
+            piece = idx[:, 32 * half : 32 * half + 32]
+            codes = keep.tile([P, BANK], U32, name="v_codes_%d" % half, align_bytes=64)
+            scales = keep.tile([P, BANK], U8, name="v_sc_%d" % half, align_bytes=64)
+            nc.vector.tensor_copy(out=codes[:], in_=table[:].indirect(piece))
+            nc.vector.tensor_copy(out=scales[:], in_=table_sc[:].indirect(piece))
+            v_codes.append(codes)
+            v_sc.append(scales)
+        nc.vector.tensor_copy(
+            out=w2_sc[:].rearrange("p (b t m) -> p b m t", b=GROUPS, t=PACK),
+            in_=w2_sc_raw[:].rearrange("p (b m t) -> p b m t", b=GROUPS, t=PACK),
+        )
+
+        grouped, w_codes, w_sc = {}, {}, {}
+
+        def round_weight(name, b, piece, copy):
+            if piece == 0:
+                grouped[name, b] = work.tile([P, PACK * PASS], BF16, name="grouped", tag="grouped", align_bytes=64)
+            dst = grouped[name, b][:].rearrange("p (t m j) -> p m j t", t=PACK, j=PACK)
+            copy(out=dst[:, 64 * piece : 64 * piece + 64, :, :], in_=raw[name, b, piece][:].rearrange("p j (m t) -> p m j t", t=PACK))
+
+        def quantize_weight(name, b):
+            codes = keep.tile([P, PASS], U32, name="codes_%s_%d" % (name, b), align_bytes=64)
+            scales = keep.tile([P, PASS], U8, name="scales_%s_%d" % (name, b), align_bytes=64)
+            nc.vector.quantize_mx(out=codes[:].bitcast(FP8X4), scales=scales[:], in_=grouped[name, b][:])
+            w_codes[name, b], w_sc[name, b] = codes, scales
+
+        def product(name, slot, half):
+            b, t = divmod(slot, PACK)
+            bank = next_bank()
+            if name == "w2":
+                lhs = w2_codes[:, 2 * P * slot : 2 * P * (slot + 1)].bitcast(FP4X4)
+                lhs_sc = w2_sc[:, P * slot : P * (slot + 1)]
+            else:
+                lhs = w_codes[name, b][:, P * t : P * (t + 1)].bitcast(FP8X4)
+                lhs_sc = w_sc[name, b][:, P * t : P * (t + 1)]
+            nc.tensor.matmul_mx(
+                out=bank[:], lhsT=lhs, lhsT_scale=lhs_sc, rhs=v_codes[half][:].bitcast(FP8X4), rhs_scale=v_sc[half][:], start=True, stop=True
+            )
+            return bank
+
+        rings, hits, bases, h, neg_top, looked, weight, page, pairs = {}, {}, {}, {}, {}, {}, {}, {}, {}
+        q_codes, q_sc, woven = {}, {}, {}
+
+        def products(slot):
+            for half in range(HALVES):
+                ring_bank = product("w2", slot, half)
+                ring = work.tile([P, BANK], F32, name="ring", tag="ring", bufs=4)
+                nc.scalar.copy(out=ring[:], in_=ring_bank[:])
+                rings[slot, half] = ring
+            for half in range(HALVES):
+                hits[slot, half] = product("w1", slot, half)
+            for half in range(HALVES):
+                bases[slot, half] = product("w3", slot, half)
+
+        def make_h(slot):
+            h[slot] = work.tile([P, S], F32, name="h", tag="h")
+            prods = []
+            for half in range(HALVES):
+                prod = work.tile([P, BANK], F32, name="prod", tag="prod")
+                nc.vector.tensor_tensor(out=prod[:], in0=hits[slot, half][:], in1=rings[slot, half][:], op=ALU.mult)
+                prods.append(prod)
+            for half in range(HALVES):
+                nc.vector.tensor_tensor(
+                    out=h[slot][:, BANK * half : BANK * (half + 1)], in0=bases[slot, half][:], in1=prods[half][:], op=ALU.add
+                )
+
+        def fill_page(slot):
+            b, t = divmod(slot, PACK)
+            page[slot] = work.tile([P, S], F32, name="page", tag="page")
+            nc.scalar.activation(out=page[slot][:], in_=h[slot][:], func=ACT.Copy, scale=skip_col[:, b, t : t + 1])
+
+        def look(slot):
+            b, t = divmod(slot, PACK)
+            neg_top[slot] = work.tile([P, 1], F32, name="neg_top", tag="neg_top")
+            nc.vector.tensor_reduce(out=neg_top[slot][:], in_=h[slot][:], axis=AX.X, op=ALU.max, negate=True)
+            looked[slot] = work.tile([P, LOOK], F32, name="looked", tag="looked")
+            nc.scalar.activation(out=looked[slot][:], in_=h[slot][:].indirect(p1[:]), func=ACT.Exp, bias=neg_top[slot][:])
+            weight[slot] = work.tile([P, LOOK], F32, name="weight", tag="weight", bufs=1)
+            nc.gpsimd.tensor_tensor(out=weight[slot][:], in0=mend_rows[b][:, t, :], in1=wgs_rows[:, t, :], op=ALU.mult)
+
+        def put(slot):
+            nc.vector.tensor_tensor(out=page[slot][:].indirect(p2[:]), in0=looked[slot][:], in1=weight[slot][:], op=ALU.mult)
+
+        def round_page(slot):
+            b, t = divmod(slot, PACK)
+            for half in range(HALVES):
+                if t == 0:
+                    pairs[b, half] = keep.tile([P, 2, BANK, 2], BF16, name="pairs_%d_%d" % (b, half))
+                nc.scalar.activation(
+                    out=pairs[b, half][:, t // 2, :, t % 2],
+                    in_=page[slot][:, BANK * half : BANK * (half + 1)],
+                    func=ACT.Copy,
+                    scale=gain_col[:, b, t : t + 1],
+                )
+
+        def weave_page(b, half, copy):
+            woven[b, half] = work.tile([P, BANK * PACK], BF16, name="woven", tag="woven", align_bytes=64)
+            copy(
+                out=woven[b, half][:].bitcast(F32).rearrange("p (c u) -> p c u", u=2),
+                in_=pairs[b, half][:].rearrange("p u c e -> p u (c e)").bitcast(F32).rearrange("p u c -> p c u"),
+            )
+
+        def quantize_page(b, half):
+            q_codes[b, half] = keep.tile([P, BANK], U32, name="q_codes_%d_%d" % (b, half), align_bytes=64)
+            q_sc[b, half] = keep.tile([P, BANK], U8, name="q_sc_%d_%d" % (b, half), align_bytes=64)
+            nc.vector.quantize_mx(out=q_codes[b, half][:].bitcast(FP8X4), scales=q_sc[b, half][:], in_=woven[b, half][:])
+
+        def last_pass(bank, n, b, half):
+            nc.tensor.matmul_mx(
+                out=bank[:],
+                lhsT=w4_codes[:, b, P * n : P * (n + 1)].bitcast(FP8X4),
+                lhsT_scale=w4_sc[:, N * b + P * n : N * b + P * (n + 1)],
+                rhs=q_codes[b, half][:].bitcast(FP8X4),
+                rhs_scale=q_sc[b, half][:],
+                start=(b == 0),
+                stop=(b == GROUPS - 1),
+            )
+
+        round_weight("w1", 0, 0, nc.scalar.copy)
+        round_weight("w1", 0, 1, nc.scalar.copy)
+        round_weight("w3", 0, 0, nc.vector.tensor_copy)
+        quantize_weight("w1", 0)
+        round_weight("w3", 0, 1, nc.vector.tensor_copy)
+        quantize_weight("w3", 0)
+        products(0)
+        make_h(0)
+        for slot in range(SLOTS):
+            if slot + 1 < SLOTS:
+                products(slot + 1)
+            fill_page(slot)
+            look(slot)
+            if slot >= 1:
+                round_page(slot - 1)
+            if slot in (1, 2):
+                name = "w1" if slot == 1 else "w3"
+                round_weight(name, 1, 0, nc.scalar.copy)
+                round_weight(name, 1, 1, nc.scalar.copy)
+            if slot in (4, 5):
+                weave_page(0, slot - 4, nc.scalar.copy)
+            if slot + 1 < SLOTS:
+                make_h(slot + 1)
+            put(slot)
+            if slot in (1, 2):
+                quantize_weight("w1" if slot == 1 else "w3", 1)
+            if slot in (4, 5):
+                quantize_page(0, slot - 4)
+
+        out_banks = {}
+        for half in range(HALVES):
+            for n in range(N // P):
+                out_banks[half, n] = next_bank()
+                last_pass(out_banks[half, n], n, 0, half)
+        round_page(SLOTS - 1)
+        for half in range(HALVES):
+            weave_page(1, half, nc.vector.tensor_copy)
+            quantize_page(1, half)
+        for half in range(HALVES):
+            for n in range(N // P):
+                last_pass(out_banks[half, n], n, 1, half)
+                result = work.tile([P, BANK], F32, name="result", tag="result", bufs=6)
+                copy = nc.vector.tensor_copy if (half, n) in ((1, 0), (1, 2)) else nc.scalar.copy
+                copy(out=result[:], in_=out_banks[half, n][:])
+                nc.sync.dma_start(out=out[P * n : P * (n + 1), BANK * half : BANK * (half + 1)], in_=result[:])

@@ -25,6 +25,8 @@ GROUPS = H // PASS
 SLOTS = GROUPS * PACK
 HALVES = S // BANK
 BANKS = 8
+QUARTER = 256
+WIDTH = (BANK, QUARTER)
 
 
 def tile_list_grainloss_window_mender_kernel(
@@ -58,14 +60,14 @@ def tile_list_grainloss_window_mender_kernel(
         w4_sc = keep.tile([P, GROUPS * N], U8, name="w4_sc", align_bytes=64)
 
         nc.vector.memset(table_sc[:].bitcast(I32), 0)
-        nc.vector.memset(w2_sc_raw[:].bitcast(I32), 0)
+        nc.gpsimd.memset(w2_sc_raw[:].bitcast(I32), 0)
         nc.vector.memset(w4_sc[:].bitcast(I32), 0)
 
-        nc.sync.dma_start(out=w2_raw[:].bitcast(I32), in_=w2_words[0].bitcast(I32))
-        load_scale_rows(nc.gpsimd, table_sc, tab_scales)
-        load_scale_rows(nc.gpsimd, w2_sc_raw, w2_scales)
-        nc.sync.dma_start(idx[:], offs)
         nc.sync.dma_start(out=table[:].bitcast(I32), in_=tab_words[0].rearrange("p t i -> p (t i)").bitcast(I32))
+        nc.sync.dma_start(idx[:], offs)
+        load_scale_rows(nc.sync, table_sc, tab_scales)
+        load_scale_rows(nc.gpsimd, w2_sc_raw, w2_scales)
+        nc.sync.dma_start(out=w2_raw[:].bitcast(I32), in_=w2_words[0].bitcast(I32))
 
         raw = {}
 
@@ -100,10 +102,15 @@ def tile_list_grainloss_window_mender_kernel(
 
         w2_codes = keep.tile([P, 2 * H], U8, name="w2_codes", align_bytes=64)
         w2_sc = keep.tile([P, H], U8, name="w2_sc", align_bytes=64)
-        nc.vector.tensor_copy(
-            out=w2_codes[:].rearrange("p (b t m e) -> p b m t e", b=GROUPS, t=PACK, e=2),
-            in_=w2_raw[:].rearrange("p (b m t e) -> p b m t e", b=GROUPS, t=PACK, e=2),
+        nc.scalar.copy(
+            out=w2_codes[:].bitcast(U16).rearrange("p (b t m) -> p b m t", b=GROUPS, t=PACK),
+            in_=w2_raw[:].bitcast(U16).rearrange("p (b m t) -> p b m t", b=GROUPS, t=PACK),
         )
+        for b in range(GROUPS):
+            nc.gpsimd.tensor_copy(
+                out=w2_sc[:, PASS * b : PASS * (b + 1)].rearrange("p (t m) -> p m t", t=PACK),
+                in_=w2_sc_raw[:, PASS * b : PASS * (b + 1)].rearrange("p (m t) -> p m t", t=PACK),
+            )
 
         v_codes, v_sc = [], []
         for half in range(HALVES):
@@ -114,10 +121,6 @@ def tile_list_grainloss_window_mender_kernel(
             nc.vector.tensor_copy(out=scales[:], in_=table_sc[:].indirect(piece))
             v_codes.append(codes)
             v_sc.append(scales)
-        nc.vector.tensor_copy(
-            out=w2_sc[:].rearrange("p (b t m) -> p b m t", b=GROUPS, t=PACK),
-            in_=w2_sc_raw[:].rearrange("p (b m t) -> p b m t", b=GROUPS, t=PACK),
-        )
 
         grouped, w_codes, w_sc = {}, {}, {}
 
@@ -184,7 +187,7 @@ def tile_list_grainloss_window_mender_kernel(
             nc.vector.tensor_reduce(out=neg_top[slot][:], in_=h[slot][:], axis=AX.X, op=ALU.max, negate=True)
             looked[slot] = work.tile([P, LOOK], F32, name="looked", tag="looked")
             nc.scalar.activation(out=looked[slot][:], in_=h[slot][:].indirect(p1[:]), func=ACT.Exp, bias=neg_top[slot][:])
-            weight[slot] = work.tile([P, LOOK], F32, name="weight", tag="weight", bufs=1)
+            weight[slot] = work.tile([P, LOOK], F32, name="weight", tag="weight")
             nc.gpsimd.tensor_tensor(out=weight[slot][:], in0=mend_rows[b][:, t, :], in1=wgs_rows[:, t, :], op=ALU.mult)
 
         def put(slot):
@@ -192,37 +195,39 @@ def tile_list_grainloss_window_mender_kernel(
 
         def round_page(slot):
             b, t = divmod(slot, PACK)
-            for half in range(HALVES):
+            width = WIDTH[b]
+            for part in range(S // width):
                 if t == 0:
-                    pairs[b, half] = keep.tile([P, 2, BANK, 2], BF16, name="pairs_%d_%d" % (b, half))
+                    pairs[b, part] = keep.tile([P, 2, width, 2], BF16, name="pairs_%d_%d" % (b, part))
                 nc.scalar.activation(
-                    out=pairs[b, half][:, t // 2, :, t % 2],
-                    in_=page[slot][:, BANK * half : BANK * (half + 1)],
+                    out=pairs[b, part][:, t // 2, :, t % 2],
+                    in_=page[slot][:, width * part : width * (part + 1)],
                     func=ACT.Copy,
                     scale=gain_col[:, b, t : t + 1],
                 )
 
-        def weave_page(b, half, copy):
-            woven[b, half] = work.tile([P, BANK * PACK], BF16, name="woven", tag="woven", align_bytes=64)
+        def weave_page(b, part, copy):
+            woven[b, part] = work.tile([P, WIDTH[b] * PACK], BF16, name="woven", tag="woven", align_bytes=64)
             copy(
-                out=woven[b, half][:].bitcast(F32).rearrange("p (c u) -> p c u", u=2),
-                in_=pairs[b, half][:].rearrange("p u c e -> p u (c e)").bitcast(F32).rearrange("p u c -> p c u"),
+                out=woven[b, part][:].bitcast(F32).rearrange("p (c u) -> p c u", u=2),
+                in_=pairs[b, part][:].rearrange("p u c e -> p u (c e)").bitcast(F32).rearrange("p u c -> p c u"),
             )
 
-        def quantize_page(b, half):
-            q_codes[b, half] = keep.tile([P, BANK], U32, name="q_codes_%d_%d" % (b, half), align_bytes=64)
-            q_sc[b, half] = keep.tile([P, BANK], U8, name="q_sc_%d_%d" % (b, half), align_bytes=64)
-            nc.vector.quantize_mx(out=q_codes[b, half][:].bitcast(FP8X4), scales=q_sc[b, half][:], in_=woven[b, half][:])
+        def quantize_page(b, part):
+            q_codes[b, part] = keep.tile([P, WIDTH[b]], U32, name="q_codes_%d_%d" % (b, part), align_bytes=64)
+            q_sc[b, part] = keep.tile([P, WIDTH[b]], U8, name="q_sc_%d_%d" % (b, part), align_bytes=64)
+            nc.vector.quantize_mx(out=q_codes[b, part][:].bitcast(FP8X4), scales=q_sc[b, part][:], in_=woven[b, part][:])
 
-        def last_pass(bank, n, b, half):
+        def last_pass(target, n, b, quarter, start, stop):
+            part, c0 = divmod(QUARTER * quarter, WIDTH[b])
             nc.tensor.matmul_mx(
-                out=bank[:],
+                out=target,
                 lhsT=w4_codes[:, b, P * n : P * (n + 1)].bitcast(FP8X4),
                 lhsT_scale=w4_sc[:, N * b + P * n : N * b + P * (n + 1)],
-                rhs=q_codes[b, half][:].bitcast(FP8X4),
-                rhs_scale=q_sc[b, half][:],
-                start=(b == 0),
-                stop=(b == GROUPS - 1),
+                rhs=q_codes[b, part][:, c0 : c0 + QUARTER].bitcast(FP8X4),
+                rhs_scale=q_sc[b, part][:, c0 : c0 + QUARTER],
+                start=start,
+                stop=stop,
             )
 
         round_weight("w1", 0, 0, nc.scalar.copy)
@@ -237,7 +242,8 @@ def tile_list_grainloss_window_mender_kernel(
             if slot + 1 < SLOTS:
                 products(slot + 1)
             fill_page(slot)
-            look(slot)
+            if slot + 1 < SLOTS:
+                look(slot)
             if slot >= 1:
                 round_page(slot - 1)
             if slot in (1, 2):
@@ -248,25 +254,43 @@ def tile_list_grainloss_window_mender_kernel(
                 weave_page(0, slot - 4, nc.scalar.copy)
             if slot + 1 < SLOTS:
                 make_h(slot + 1)
+            if slot + 2 == SLOTS:
+                look(slot + 1)
             put(slot)
             if slot in (1, 2):
                 quantize_weight("w1" if slot == 1 else "w3", 1)
             if slot in (4, 5):
                 quantize_page(0, slot - 4)
 
-        out_banks = {}
-        for half in range(HALVES):
-            for n in range(N // P):
-                out_banks[half, n] = next_bank()
-                last_pass(out_banks[half, n], n, 0, half)
+        front, back = {}, {}
+        for quarter in range(S // QUARTER):
+            front[quarter] = next_bank()
+            if quarter % 2 == 0:
+                back[quarter // 2] = next_bank()
+            for n in range(2):
+                last_pass(front[quarter][:, QUARTER * n : QUARTER * (n + 1)], n, 0, quarter, n == 0, False)
+            side = quarter % 2
+            last_pass(back[quarter // 2][:, QUARTER * side : QUARTER * (side + 1)], 2, 0, quarter, side == 0, False)
         round_page(SLOTS - 1)
-        for half in range(HALVES):
-            weave_page(1, half, nc.vector.tensor_copy)
-            quantize_page(1, half)
-        for half in range(HALVES):
-            for n in range(N // P):
-                last_pass(out_banks[half, n], n, 1, half)
+        weave_page(1, 0, nc.vector.tensor_copy)
+        for quarter in range(S // QUARTER):
+            if quarter + 1 < S // QUARTER:
+                weave_page(1, quarter + 1, nc.vector.tensor_copy)
+            quantize_page(1, quarter)
+        for quarter in range(S // QUARTER):
+            side = quarter % 2
+            last_pass(back[quarter // 2][:, QUARTER * side : QUARTER * (side + 1)], 2, 1, quarter, False, side == 1)
+            for n in range(2):
+                last_pass(front[quarter][:, QUARTER * n : QUARTER * (n + 1)], n, 1, quarter, False, n == 1)
+            if side == 1:
                 result = work.tile([P, BANK], F32, name="result", tag="result", bufs=6)
-                copy = nc.vector.tensor_copy if (half, n) in ((1, 0), (1, 2)) else nc.scalar.copy
-                copy(out=result[:], in_=out_banks[half, n][:])
-                nc.sync.dma_start(out=out[P * n : P * (n + 1), BANK * half : BANK * (half + 1)], in_=result[:])
+                copy = nc.scalar.copy if quarter == 1 else nc.vector.tensor_copy
+                copy(out=result[:], in_=back[quarter // 2][:])
+                nc.sync.dma_start(out=out[2 * P : 3 * P, BANK * (quarter // 2) : BANK * (quarter // 2 + 1)], in_=result[:])
+            result = work.tile([P, BANK], F32, name="result", tag="result", bufs=6)
+            copy = nc.vector.tensor_copy if quarter == 2 else nc.scalar.copy
+            copy(out=result[:], in_=front[quarter][:])
+            nc.sync.dma_start(
+                out=out[0 : 2 * P, QUARTER * quarter : QUARTER * (quarter + 1)].rearrange("(n p) c -> p n c", n=2),
+                in_=result[:].rearrange("p (n c) -> p n c", n=2),
+            )

@@ -25,6 +25,7 @@ GROUPS = H // PASS
 SLOTS = GROUPS * PACK
 HALVES = S // BANK
 BANKS = 8
+FIRST_TENANT = {("w1", 0, 1): "first0", ("w3", 0, 1): "first1", ("w3", 0, 0): "second0"}
 QUARTER = 256
 WIDTH = (BANK, QUARTER)
 
@@ -52,9 +53,8 @@ def tile_list_grainloss_window_mender_kernel(
         idx = keep.tile([P, S // 16], U16, name="idx")
         p1 = keep.tile([P, LOOK // 16], U16, name="p1")
         p2 = keep.tile([P, LOOK // 16], U16, name="p2")
-        table = keep.tile([P, T], U32, name="table", align_bytes=64)
+        table = keep.tile([P, T], U32, name="table", tag="table", align_bytes=64)
         table_sc = keep.tile([P, T], U8, name="table_sc", align_bytes=64)
-        w2_raw = keep.tile([P, 2 * H], U8, name="w2_raw", align_bytes=64)
         w2_sc_raw = keep.tile([P, H], U8, name="w2_sc_raw", align_bytes=64)
         w4_codes = keep.tile([P, GROUPS, N], U32, name="w4_codes", align_bytes=64)
         w4_sc = keep.tile([P, GROUPS * N], U8, name="w4_sc", align_bytes=64)
@@ -63,18 +63,27 @@ def tile_list_grainloss_window_mender_kernel(
         nc.gpsimd.memset(w2_sc_raw[:].bitcast(I32), 0)
         nc.vector.memset(w4_sc[:].bitcast(I32), 0)
 
+        w2_raw = []
+        for b in range(GROUPS):
+            tile = keep.tile([P, 2 * PASS], U8, name="w2_raw_%d" % b, align_bytes=64)
+            w2_raw.append(tile)
+
+        def load_w2_words(b):
+            nc.sync.dma_start(out=w2_raw[b][:].bitcast(I32), in_=w2_words[0][:, 2 * PASS * b : 2 * PASS * (b + 1)].bitcast(I32))
+
         nc.sync.dma_start(out=table[:].bitcast(I32), in_=tab_words[0].rearrange("p t i -> p (t i)").bitcast(I32))
         nc.sync.dma_start(idx[:], offs)
         load_scale_rows(nc.sync, table_sc, tab_scales)
         load_scale_rows(nc.gpsimd, w2_sc_raw, w2_scales)
-        nc.sync.dma_start(out=w2_raw[:].bitcast(I32), in_=w2_words[0].bitcast(I32))
+        load_w2_words(0)
 
         raw = {}
 
         def load_weight(name, w, b):
             for piece in range(2):
                 c0 = PASS * b + 256 * piece
-                tile = keep.tile([P, PACK, 256], F32, name="raw_%s_%d_%d" % (name, b, piece))
+                tag = FIRST_TENANT.get((name, b, piece), "raw_%s_%d_%d" % (name, b, piece))
+                tile = keep.tile([P, PACK, 256], F32, name="raw", tag=tag, align_bytes=64)
                 nc.sync.dma_start(out=tile[:], in_=w[:, c0 : c0 + 256].rearrange("(p j) c -> p j c", j=PACK))
                 raw[name, b, piece] = tile
 
@@ -89,28 +98,32 @@ def tile_list_grainloss_window_mender_kernel(
         wgs_rows = keep.tile([P, PACK, LOOK], F32, name="wgs_rows")
         for q in range(4):
             nc.sync.dma_start(out=wgs_rows[32 * q : 32 * q + 32, :, :], in_=wgs.rearrange("(x t) m -> x t m", t=PACK))
-        mend_rows = []
-        for b in range(GROUPS):
-            tile = keep.tile([P, PACK, LOOK], F32, name="mend_%d" % b)
-            mend_rows.append(tile)
-        nc.sync.dma_start(out=mend_rows[0][:], in_=mend[0:PASS, :].rearrange("(p t) m -> p t m", t=PACK))
+        mend_rows = {}
+
+        def load_mend(b, t0, t1):
+            tile = keep.tile([P, t1 - t0, LOOK], F32, name="mend_%d_%d" % (b, t0))
+            rows = mend[PASS * b : PASS * (b + 1), :].rearrange("(p t) m -> p t m", t=PACK)
+            nc.sync.dma_start(out=tile[:], in_=rows[:, t0:t1, :])
+            for t in range(t0, t1):
+                mend_rows[PACK * b + t] = tile[:, t - t0, :]
+
+        load_mend(0, 0, 1)
         load_weight("w1", w1, 1)
+        load_mend(0, 1, PACK)
+        load_w2_words(1)
         load_weight("w3", w3, 1)
-        nc.sync.dma_start(out=mend_rows[1][:], in_=mend[PASS : 2 * PASS, :].rearrange("(p t) m -> p t m", t=PACK))
+        load_mend(1, 0, PACK)
         nc.sync.dma_start(out=w4_codes[:].bitcast(I32), in_=w4_words.rearrange("a p c i -> p a (c i)").bitcast(I32))
         load_scale_rows(nc.sync, w4_sc, w4_scales)
 
-        w2_codes = keep.tile([P, 2 * H], U8, name="w2_codes", align_bytes=64)
-        w2_sc = keep.tile([P, H], U8, name="w2_sc", align_bytes=64)
-        nc.scalar.copy(
-            out=w2_codes[:].bitcast(U16).rearrange("p (b t m) -> p b m t", b=GROUPS, t=PACK),
-            in_=w2_raw[:].bitcast(U16).rearrange("p (b m t) -> p b m t", b=GROUPS, t=PACK),
-        )
-        for b in range(GROUPS):
-            nc.gpsimd.tensor_copy(
-                out=w2_sc[:, PASS * b : PASS * (b + 1)].rearrange("p (t m) -> p m t", t=PACK),
-                in_=w2_sc_raw[:, PASS * b : PASS * (b + 1)].rearrange("p (m t) -> p m t", t=PACK),
+        w2_codes = [keep.tile([P, 2 * PASS], U8, name="w2_codes_%d" % b, align_bytes=64) for b in range(GROUPS)]
+        def deal_w2_words(b):
+            nc.scalar.copy(
+                out=w2_codes[b][:].bitcast(U16).rearrange("p (t m) -> p m t", t=PACK),
+                in_=w2_raw[b][:].bitcast(U16).rearrange("p (m t) -> p m t", t=PACK),
             )
+
+        deal_w2_words(0)
 
         v_codes, v_sc = [], []
         for half in range(HALVES):
@@ -118,15 +131,23 @@ def tile_list_grainloss_window_mender_kernel(
             codes = keep.tile([P, BANK], U32, name="v_codes_%d" % half, align_bytes=64)
             scales = keep.tile([P, BANK], U8, name="v_sc_%d" % half, align_bytes=64)
             nc.vector.tensor_copy(out=codes[:], in_=table[:].indirect(piece))
-            nc.vector.tensor_copy(out=scales[:], in_=table_sc[:].indirect(piece))
             v_codes.append(codes)
             v_sc.append(scales)
+        for half in range(HALVES):
+            nc.vector.tensor_copy(out=v_sc[half][:], in_=table_sc[:].indirect(idx[:, 32 * half : 32 * half + 32]))
+
+        w2_sc = keep.tile([P, H], U8, name="w2_sc", tag="table", align_bytes=64)
+        nc.vector.tensor_copy(
+            out=w2_sc[:].rearrange("p (b t m) -> p b m t", b=GROUPS, t=PACK),
+            in_=w2_sc_raw[:].rearrange("p (b m t) -> p b m t", b=GROUPS, t=PACK),
+        )
 
         grouped, w_codes, w_sc = {}, {}, {}
 
         def round_weight(name, b, piece, copy):
             if piece == 0:
-                grouped[name, b] = work.tile([P, PACK * PASS], BF16, name="grouped", tag="grouped", align_bytes=64)
+                tag = "second1" if (name, b) == ("w1", 0) else "grouped_%s" % name
+                grouped[name, b] = keep.tile([P, PACK * PASS], BF16, name="grouped", tag=tag, align_bytes=64)
             dst = grouped[name, b][:].rearrange("p (t m j) -> p m j t", t=PACK, j=PACK)
             copy(out=dst[:, 64 * piece : 64 * piece + 64, :, :], in_=raw[name, b, piece][:].rearrange("p j (m t) -> p m j t", t=PACK))
 
@@ -140,7 +161,7 @@ def tile_list_grainloss_window_mender_kernel(
             b, t = divmod(slot, PACK)
             bank = next_bank()
             if name == "w2":
-                lhs = w2_codes[:, 2 * P * slot : 2 * P * (slot + 1)].bitcast(FP4X4)
+                lhs = w2_codes[b][:, 2 * P * t : 2 * P * (t + 1)].bitcast(FP4X4)
                 lhs_sc = w2_sc[:, P * slot : P * (slot + 1)]
             else:
                 lhs = w_codes[name, b][:, P * t : P * (t + 1)].bitcast(FP8X4)
@@ -153,12 +174,14 @@ def tile_list_grainloss_window_mender_kernel(
         rings, hits, bases, h, neg_top, looked, weight, page, pairs = {}, {}, {}, {}, {}, {}, {}, {}, {}
         q_codes, q_sc, woven = {}, {}, {}
 
-        def products(slot):
+        def ring_products(slot):
             for half in range(HALVES):
                 ring_bank = product("w2", slot, half)
-                ring = work.tile([P, BANK], F32, name="ring", tag="ring", bufs=4)
-                nc.scalar.copy(out=ring[:], in_=ring_bank[:])
-                rings[slot, half] = ring
+                tag = "first%d" % (slot % 3) if half == 0 else "second%d" % (slot % 2)
+                rings[slot, half] = keep.tile([P, BANK], F32, name="ring", tag=tag, align_bytes=64)
+                nc.scalar.copy(out=rings[slot, half][:], in_=ring_bank[:])
+
+        def products(slot):
             for half in range(HALVES):
                 hits[slot, half] = product("w1", slot, half)
             for half in range(HALVES):
@@ -176,19 +199,21 @@ def tile_list_grainloss_window_mender_kernel(
                     out=h[slot][:, BANK * half : BANK * (half + 1)], in0=bases[slot, half][:], in1=prods[half][:], op=ALU.add
                 )
 
+
+        def make_weight(slot, tag):
+            weight[slot] = keep.tile([P, LOOK], F32, name="weight", tag=tag, align_bytes=64)
+            nc.gpsimd.tensor_tensor(out=weight[slot][:], in0=mend_rows[slot], in1=wgs_rows[:, slot % PACK, :], op=ALU.mult)
+
         def fill_page(slot):
             b, t = divmod(slot, PACK)
-            page[slot] = work.tile([P, S], F32, name="page", tag="page")
+            page[slot] = work.tile([P, S], F32, name="page", tag="page", bufs=3)
             nc.scalar.activation(out=page[slot][:], in_=h[slot][:], func=ACT.Copy, scale=skip_col[:, b, t : t + 1])
 
         def look(slot):
-            b, t = divmod(slot, PACK)
             neg_top[slot] = work.tile([P, 1], F32, name="neg_top", tag="neg_top")
             nc.vector.tensor_reduce(out=neg_top[slot][:], in_=h[slot][:], axis=AX.X, op=ALU.max, negate=True)
             looked[slot] = work.tile([P, LOOK], F32, name="looked", tag="looked")
             nc.scalar.activation(out=looked[slot][:], in_=h[slot][:].indirect(p1[:]), func=ACT.Exp, bias=neg_top[slot][:])
-            weight[slot] = work.tile([P, LOOK], F32, name="weight", tag="weight")
-            nc.gpsimd.tensor_tensor(out=weight[slot][:], in0=mend_rows[b][:, t, :], in1=wgs_rows[:, t, :], op=ALU.mult)
 
         def put(slot):
             nc.vector.tensor_tensor(out=page[slot][:].indirect(p2[:]), in0=looked[slot][:], in1=weight[slot][:], op=ALU.mult)
@@ -234,28 +259,37 @@ def tile_list_grainloss_window_mender_kernel(
         round_weight("w1", 0, 1, nc.scalar.copy)
         round_weight("w3", 0, 0, nc.vector.tensor_copy)
         quantize_weight("w1", 0)
-        round_weight("w3", 0, 1, nc.vector.tensor_copy)
+        round_weight("w3", 0, 1, nc.scalar.copy)
         quantize_weight("w3", 0)
+        ring_products(0)
         products(0)
         make_h(0)
+        make_weight(0, "first0")
+        late_rounds = {0: (("w1", 0), ("w1", 1)), 1: (("w3", 0),), 2: (("w3", 1),)}
         for slot in range(SLOTS):
             if slot + 1 < SLOTS:
+                ring_products(slot + 1)
                 products(slot + 1)
             fill_page(slot)
             if slot + 1 < SLOTS:
                 look(slot)
             if slot >= 1:
                 round_page(slot - 1)
-            if slot in (1, 2):
-                name = "w1" if slot == 1 else "w3"
-                round_weight(name, 1, 0, nc.scalar.copy)
-                round_weight(name, 1, 1, nc.scalar.copy)
+            for name, piece in late_rounds.get(slot, ()):
+                round_weight(name, 1, piece, nc.scalar.copy)
+            if slot == 1:
+                deal_w2_words(1)
             if slot in (4, 5):
                 weave_page(0, slot - 4, nc.scalar.copy)
             if slot + 1 < SLOTS:
                 make_h(slot + 1)
+            if slot + 3 < SLOTS:
+                make_weight(slot + 1, "first%d" % ((slot + 1) % 3))
+            if slot + 3 == SLOTS:
+                make_weight(slot + 2, "first%d" % ((slot + 1) % 3))
             if slot + 2 == SLOTS:
                 look(slot + 1)
+                make_weight(slot, "second%d" % ((slot + 1) % 2))
             put(slot)
             if slot in (1, 2):
                 quantize_weight("w1" if slot == 1 else "w3", 1)

from contextlib import ExitStack

import concourse.mybir as mybir

K, T, S, LOOK, H, N = 512, 4096, 1024, 512, 1024, 384
FLOPS = 2 * (3 * K * H * S + H * N * S)

F32 = mybir.dt.float32
BF16 = mybir.dt.bfloat16
I32 = mybir.dt.int32
U32 = mybir.dt.uint32
U16 = mybir.dt.uint16
U8 = mybir.dt.uint8
FP8X4 = mybir.dt.float8_e4m3fn_x4
FP4X4 = mybir.dt.float4_e2m1fn_x4
ALU = mybir.AluOpType
ACT = mybir.ActivationFunctionType
AX = mybir.AxisListType

P = 128
PACK = 4
PASS = P * PACK
BANK = 512
GROUPS = H // PASS
SLOTS = GROUPS * PACK
HALVES = S // BANK
BANKS = 8
FIRST_TENANT = {("w1", 0, 1): "first0", ("w3", 0, 1): "first1", ("w3", 0, 0): "second0"}
QUARTER = 256
WIDTH = (BANK, QUARTER)


def tile_list_grainloss_window_mender_kernel(
    tc, tab_words, tab_scales, offs, pos1, pos2, w1, w2_words, w2_scales, w3, mend, skip, wgs, gain, w4_words, w4_scales, out
):
    nc = tc.nc
    with ExitStack() as ctx:
        keep = ctx.enter_context(tc.tile_pool(name="keep", bufs=1))
        work = ctx.enter_context(tc.tile_pool(name="work", bufs=2))
        psum = ctx.enter_context(tc.psum_pool(name="psum", bufs=1))
        bank_turn = []

        def next_bank():
            tag = "bank%d" % (len(bank_turn) % BANKS)
            bank_turn.append(tag)
            return psum.tile([P, BANK], F32, name=tag, tag=tag)

        def load_scale_rows(queue, plane, rows):
            by_row = rows.rearrange("a (Q r) c -> r Q a c", r=4)
            for r in range(4):
                queue.dma_start(out=plane[r:P:32, :].rearrange("p (a c) -> p a c", a=rows.shape[0]).bitcast(I32), in_=by_row[r].bitcast(I32))

        idx = keep.tile([P, S // 16], U16, name="idx")
        p1 = keep.tile([P, LOOK // 16], U16, name="p1")
        p2 = keep.tile([P, LOOK // 16], U16, name="p2")
        table = keep.tile([P, T], U32, name="table", tag="table", align_bytes=64)
        table_sc = keep.tile([P, T], U8, name="table_sc", align_bytes=64)
        w2_sc_raw = keep.tile([P, H], U8, name="w2_sc_raw", align_bytes=64)
        w4_codes = keep.tile([P, GROUPS, N], U32, name="w4_codes", align_bytes=64)
        w4_sc = keep.tile([P, GROUPS * N], U8, name="w4_sc", align_bytes=64)

        nc.vector.memset(table_sc[:].bitcast(I32), 0)
        nc.gpsimd.memset(w2_sc_raw[:].bitcast(I32), 0)
        nc.vector.memset(w4_sc[:].bitcast(I32), 0)

        w2_raw = []
        for b in range(GROUPS):
            tile = keep.tile([P, 2 * PASS], U8, name="w2_raw_%d" % b, align_bytes=64)
            w2_raw.append(tile)

        def load_w2_words(b):
            nc.sync.dma_start(out=w2_raw[b][:].bitcast(I32), in_=w2_words[0][:, 2 * PASS * b : 2 * PASS * (b + 1)].bitcast(I32))

        nc.sync.dma_start(out=table[:].bitcast(I32), in_=tab_words[0].rearrange("p t i -> p (t i)").bitcast(I32))
        nc.sync.dma_start(idx[:], offs)
        load_scale_rows(nc.sync, table_sc, tab_scales)
        load_scale_rows(nc.gpsimd, w2_sc_raw, w2_scales)
        load_w2_words(0)

        raw = {}

        def load_weight(name, w, b):
            for piece in range(2):
                c0 = PASS * b + 256 * piece
                tag = FIRST_TENANT.get((name, b, piece), "raw_%s_%d_%d" % (name, b, piece))
                tile = keep.tile([P, PACK, 256], F32, name="raw", tag=tag, align_bytes=64)
                nc.sync.dma_start(out=tile[:], in_=w[:, c0 : c0 + 256].rearrange("(p j) c -> p j c", j=PACK))
                raw[name, b, piece] = tile

        load_weight("w1", w1, 0)
        load_weight("w3", w3, 0)
        nc.sync.dma_start(p1[:], pos1)
        nc.sync.dma_start(p2[:], pos2)
        skip_col = keep.tile([P, GROUPS, PACK], F32, name="skip_col")
        gain_col = keep.tile([P, GROUPS, PACK], F32, name="gain_col")
        nc.sync.dma_start(out=skip_col[:], in_=skip.rearrange("(b p t) -> p b t", b=GROUPS, t=PACK))
        nc.sync.dma_start(out=gain_col[:], in_=gain.rearrange("(b p t) -> p b t", b=GROUPS, t=PACK))
        wgs_rows = keep.tile([P, PACK, LOOK], F32, name="wgs_rows")
        for q in range(4):
            nc.sync.dma_start(out=wgs_rows[32 * q : 32 * q + 32, :, :], in_=wgs.rearrange("(x t) m -> x t m", t=PACK))
        mend_rows = {}

        def load_mend(b, t0, t1):
            tile = keep.tile([P, t1 - t0, LOOK], F32, name="mend_%d_%d" % (b, t0))
            rows = mend[PASS * b : PASS * (b + 1), :].rearrange("(p t) m -> p t m", t=PACK)
            nc.sync.dma_start(out=tile[:], in_=rows[:, t0:t1, :])
            for t in range(t0, t1):
                mend_rows[PACK * b + t] = tile[:, t - t0, :]

        load_mend(0, 0, 1)
        load_weight("w1", w1, 1)
        load_mend(0, 1, PACK)
        load_w2_words(1)
        load_weight("w3", w3, 1)
        load_mend(1, 0, PACK)
        nc.sync.dma_start(out=w4_codes[:].bitcast(I32), in_=w4_words.rearrange("a p c i -> p a (c i)").bitcast(I32))
        load_scale_rows(nc.sync, w4_sc, w4_scales)

        w2_codes = [keep.tile([P, 2 * PASS], U8, name="w2_codes_%d" % b, align_bytes=64) for b in range(GROUPS)]
        def deal_w2_words(b):
            nc.scalar.copy(
                out=w2_codes[b][:].bitcast(U16).rearrange("p (t m) -> p m t", t=PACK),
                in_=w2_raw[b][:].bitcast(U16).rearrange("p (m t) -> p m t", t=PACK),
            )

        deal_w2_words(0)

        v_codes, v_sc = [], []
        for half in range(HALVES):
            piece = idx[:, 32 * half : 32 * half + 32]
            codes = keep.tile([P, BANK], U32, name="v_codes_%d" % half, align_bytes=64)
            scales = keep.tile([P, BANK], U8, name="v_sc_%d" % half, align_bytes=64)
            nc.vector.tensor_copy(out=codes[:], in_=table[:].indirect(piece))
            v_codes.append(codes)
            v_sc.append(scales)
        for half in range(HALVES):
            nc.vector.tensor_copy(out=v_sc[half][:], in_=table_sc[:].indirect(idx[:, 32 * half : 32 * half + 32]))

        w2_sc = keep.tile([P, H], U8, name="w2_sc", tag="table", align_bytes=64)
        nc.vector.tensor_copy(
            out=w2_sc[:].rearrange("p (b t m) -> p b m t", b=GROUPS, t=PACK),
            in_=w2_sc_raw[:].rearrange("p (b m t) -> p b m t", b=GROUPS, t=PACK),
        )

        grouped, w_codes, w_sc = {}, {}, {}

        def round_weight(name, b, piece, copy):
            if piece == 0:
                tag = "second1" if (name, b) == ("w1", 0) else "grouped_%s" % name
                grouped[name, b] = keep.tile([P, PACK * PASS], BF16, name="grouped", tag=tag, align_bytes=64)
            dst = grouped[name, b][:].rearrange("p (t m j) -> p m j t", t=PACK, j=PACK)
            copy(out=dst[:, 64 * piece : 64 * piece + 64, :, :], in_=raw[name, b, piece][:].rearrange("p j (m t) -> p m j t", t=PACK))

        def quantize_weight(name, b):
            codes = keep.tile([P, PASS], U32, name="codes_%s_%d" % (name, b), align_bytes=64)
            scales = keep.tile([P, PASS], U8, name="scales_%s_%d" % (name, b), align_bytes=64)
            nc.vector.quantize_mx(out=codes[:].bitcast(FP8X4), scales=scales[:], in_=grouped[name, b][:])
            w_codes[name, b], w_sc[name, b] = codes, scales

        def product(name, slot, half):
            b, t = divmod(slot, PACK)
            bank = next_bank()
            if name == "w2":
                lhs = w2_codes[b][:, 2 * P * t : 2 * P * (t + 1)].bitcast(FP4X4)
                lhs_sc = w2_sc[:, P * slot : P * (slot + 1)]
            else:
                lhs = w_codes[name, b][:, P * t : P * (t + 1)].bitcast(FP8X4)
                lhs_sc = w_sc[name, b][:, P * t : P * (t + 1)]
            nc.tensor.matmul_mx(
                out=bank[:], lhsT=lhs, lhsT_scale=lhs_sc, rhs=v_codes[half][:].bitcast(FP8X4), rhs_scale=v_sc[half][:], start=True, stop=True
            )
            return bank

        rings, hits, bases, h, neg_top, looked, weight, page, pairs = {}, {}, {}, {}, {}, {}, {}, {}, {}
        q_codes, q_sc, woven = {}, {}, {}

        def ring_products(slot):
            for half in range(HALVES):
                ring_bank = product("w2", slot, half)
                tag = "first%d" % (slot % 3) if half == 0 else "second%d" % (slot % 2)
                rings[slot, half] = keep.tile([P, BANK], F32, name="ring", tag=tag, align_bytes=64)
                nc.scalar.copy(out=rings[slot, half][:], in_=ring_bank[:])

        def products(slot):
            for half in range(HALVES):
                hits[slot, half] = product("w1", slot, half)
            for half in range(HALVES):
                bases[slot, half] = product("w3", slot, half)

        def make_h(slot):
            h[slot] = work.tile([P, S], F32, name="h", tag="h")
            prods = []
            for half in range(HALVES):
                prod = work.tile([P, BANK], F32, name="prod", tag="prod")
                nc.vector.tensor_tensor(out=prod[:], in0=hits[slot, half][:], in1=rings[slot, half][:], op=ALU.mult)
                prods.append(prod)
            for half in range(HALVES):
                nc.vector.tensor_tensor(
                    out=h[slot][:, BANK * half : BANK * (half + 1)], in0=bases[slot, half][:], in1=prods[half][:], op=ALU.add
                )


        def make_weight(slot, tag):
            weight[slot] = keep.tile([P, LOOK], F32, name="weight", tag=tag, align_bytes=64)
            nc.gpsimd.tensor_tensor(out=weight[slot][:], in0=mend_rows[slot], in1=wgs_rows[:, slot % PACK, :], op=ALU.mult)

        def fill_page(slot):
            b, t = divmod(slot, PACK)
            page[slot] = work.tile([P, S], F32, name="page", tag="page", bufs=3)
            nc.scalar.activation(out=page[slot][:], in_=h[slot][:], func=ACT.Copy, scale=skip_col[:, b, t : t + 1])

        def look(slot):
            neg_top[slot] = work.tile([P, 1], F32, name="neg_top", tag="neg_top")
            nc.vector.tensor_reduce(out=neg_top[slot][:], in_=h[slot][:], axis=AX.X, op=ALU.max, negate=True)
            looked[slot] = work.tile([P, LOOK], F32, name="looked", tag="looked")
            nc.scalar.activation(out=looked[slot][:], in_=h[slot][:].indirect(p1[:]), func=ACT.Exp, bias=neg_top[slot][:])

        def put(slot):
            nc.vector.tensor_tensor(out=page[slot][:].indirect(p2[:]), in0=looked[slot][:], in1=weight[slot][:], op=ALU.mult)

        def round_page(slot):
            b, t = divmod(slot, PACK)
            width = WIDTH[b]
            for part in range(S // width):
                if t == 0:
                    pairs[b, part] = keep.tile([P, 2, width, 2], BF16, name="pairs_%d_%d" % (b, part))
                nc.scalar.activation(
                    out=pairs[b, part][:, t // 2, :, t % 2],
                    in_=page[slot][:, width * part : width * (part + 1)],
                    func=ACT.Copy,
                    scale=gain_col[:, b, t : t + 1],
                )

        def weave_page(b, part, copy):
            woven[b, part] = work.tile([P, WIDTH[b] * PACK], BF16, name="woven", tag="woven", align_bytes=64)
            copy(
                out=woven[b, part][:].bitcast(F32).rearrange("p (c u) -> p c u", u=2),
                in_=pairs[b, part][:].rearrange("p u c e -> p u (c e)").bitcast(F32).rearrange("p u c -> p c u"),
            )

        def quantize_page(b, part):
            q_codes[b, part] = keep.tile([P, WIDTH[b]], U32, name="q_codes_%d_%d" % (b, part), align_bytes=64)
            q_sc[b, part] = keep.tile([P, WIDTH[b]], U8, name="q_sc_%d_%d" % (b, part), align_bytes=64)
            nc.vector.quantize_mx(out=q_codes[b, part][:].bitcast(FP8X4), scales=q_sc[b, part][:], in_=woven[b, part][:])

        def last_pass(target, n, b, quarter, start, stop):
            part, c0 = divmod(QUARTER * quarter, WIDTH[b])
            nc.tensor.matmul_mx(
                out=target,
                lhsT=w4_codes[:, b, P * n : P * (n + 1)].bitcast(FP8X4),
                lhsT_scale=w4_sc[:, N * b + P * n : N * b + P * (n + 1)],
                rhs=q_codes[b, part][:, c0 : c0 + QUARTER].bitcast(FP8X4),
                rhs_scale=q_sc[b, part][:, c0 : c0 + QUARTER],
                start=start,
                stop=stop,
            )

        round_weight("w1", 0, 0, nc.scalar.copy)
        round_weight("w1", 0, 1, nc.scalar.copy)
        round_weight("w3", 0, 0, nc.vector.tensor_copy)
        quantize_weight("w1", 0)
        round_weight("w3", 0, 1, nc.scalar.copy)
        quantize_weight("w3", 0)
        ring_products(0)
        products(0)
        make_h(0)
        make_weight(0, "first0")
        late_rounds = {0: (("w1", 0), ("w1", 1)), 1: (("w3", 0),), 2: (("w3", 1),)}
        for slot in range(SLOTS):
            if slot + 1 < SLOTS:
                ring_products(slot + 1)
                products(slot + 1)
            fill_page(slot)
            if slot + 1 < SLOTS:
                look(slot)
            if slot >= 1:
                round_page(slot - 1)
            for name, piece in late_rounds.get(slot, ()):
                round_weight(name, 1, piece, nc.scalar.copy)
            if slot == 1:
                deal_w2_words(1)
            if slot in (4, 5):
                weave_page(0, slot - 4, nc.scalar.copy)
            if slot + 1 < SLOTS:
                make_h(slot + 1)
            if slot + 3 < SLOTS:
                make_weight(slot + 1, "first%d" % ((slot + 1) % 3))
            if slot + 3 == SLOTS:
                make_weight(slot + 2, "first%d" % ((slot + 1) % 3))
            if slot + 2 == SLOTS:
                look(slot + 1)
                make_weight(slot, "second%d" % ((slot + 1) % 2))
            put(slot)
            if slot in (1, 2):
                quantize_weight("w1" if slot == 1 else "w3", 1)
            if slot in (4, 5):
                quantize_page(0, slot - 4)

        front, back = {}, {}
        for quarter in range(S // QUARTER):
            front[quarter] = next_bank()
            if quarter % 2 == 0:
                back[quarter // 2] = next_bank()
            for n in range(2):
                last_pass(front[quarter][:, QUARTER * n : QUARTER * (n + 1)], n, 0, quarter, n == 0, False)
            side = quarter % 2
            last_pass(back[quarter // 2][:, QUARTER * side : QUARTER * (side + 1)], 2, 0, quarter, side == 0, False)
        round_page(SLOTS - 1)
        weave_page(1, 0, nc.vector.tensor_copy)
        for quarter in range(S // QUARTER):
            if quarter + 1 < S // QUARTER:
                weave_page(1, quarter + 1, nc.vector.tensor_copy)
            quantize_page(1, quarter)
        for quarter in range(S // QUARTER):
            side = quarter % 2
            last_pass(back[quarter // 2][:, QUARTER * side : QUARTER * (side + 1)], 2, 1, quarter, False, side == 1)
            for n in range(2):
                last_pass(front[quarter][:, QUARTER * n : QUARTER * (n + 1)], n, 1, quarter, False, n == 1)
            if side == 1:
                result = work.tile([P, BANK], F32, name="result", tag="result", bufs=6)
                copy = nc.scalar.copy if quarter == 1 else nc.vector.tensor_copy
                copy(out=result[:], in_=back[quarter // 2][:])
                nc.sync.dma_start(out=out[2 * P : 3 * P, BANK * (quarter // 2) : BANK * (quarter // 2 + 1)], in_=result[:])
            result = work.tile([P, BANK], F32, name="result", tag="result", bufs=6)
            copy = nc.vector.tensor_copy if quarter == 2 else nc.scalar.copy
            copy(out=result[:], in_=front[quarter][:])
            nc.sync.dma_start(
                out=out[0 : 2 * P, QUARTER * quarter : QUARTER * (quarter + 1)].rearrange("(n p) c -> p n c", n=2),
                in_=result[:].rearrange("p (n c) -> p n c", n=2),
            )
